import numpy as np
import ml_dtypes


def mxq(x, axis, fmt="e4m3"):
    dtype, down = {"e4m3": (ml_dtypes.float8_e4m3fn, 7), "e5m2": (ml_dtypes.float8_e5m2, 14)}[fmt]
    v = np.moveaxis(np.asarray(x, np.float32).astype(ml_dtypes.bfloat16).astype(np.float64), axis, -1)
    blocks = v.reshape(v.shape[:-1] + (-1, 32))
    amax = np.abs(blocks).max(-1, keepdims=True)
    byte = np.maximum(np.where(amax > 0, np.frexp(amax)[1] - 1 + 127, 0) - down, 1)
    scale = np.exp2(byte - 127.0)
    codes = (blocks / scale).astype(np.float32).astype(dtype).astype(np.float64)
    return np.moveaxis((codes * scale).reshape(v.shape), -1, axis)


WIDE = False


def mx_kscale(k):
    if not WIDE:
        return np.ones(k)
    levels = np.array([10, -10, 5, -5, 0])
    if k % 512:
        return np.exp2(np.random.permutation(np.resize(levels, k // 32))).repeat(32)
    a = np.empty((k // 512, 16))
    for p in range(k // 512):
        a[p, :8] = np.random.permutation(np.resize(levels, 8))
        for g in range(8):
            far = levels[np.abs(levels - a[p, g]) >= 10]
            a[p, g + 8] = far[np.random.randint(len(far))]
    return np.exp2(a.ravel()).repeat(32)


def f64(x):
    return np.asarray(x).astype(np.float64)


def striped(idx):
    return np.tile(idx.reshape(-1, 16).T, (8, 1)).astype(np.uint16)


def unstriped(offs):
    return offs[:16].T.reshape(-1).astype(np.int64)


E2M1 = np.array([0.0, 0.5, 1.0, 1.5, 2.0, 3.0, 4.0, 6.0, -0.0, -0.5, -1.0, -1.5, -2.0, -3.0, -4.0, -6.0])


def pack_weight(w, fmt):
    k, n = w.shape
    w = f64(np.asarray(w, np.float32).astype(ml_dtypes.bfloat16)).reshape(k // 32, 32, n)
    amax = np.abs(w).max(1)
    if fmt == "e4m3":
        byte = np.frexp(amax)[1] - 1 + 127 - 7
    else:
        mant, ex = np.frexp(amax / 6.0)
        byte = np.where(mant > 0.5, ex, ex - 1) + 127
    byte = np.clip(np.where(amax > 0, byte, 1), 1, 254)
    scaled = (w * np.exp2(127.0 - byte)[:, None, :]).reshape(k, n).astype(np.float32)
    by_word = np.ascontiguousarray(scaled.reshape(k // 512, 128, 4, n).transpose(0, 1, 3, 2))
    if fmt == "e4m3":
        words = by_word.astype(ml_dtypes.float8_e4m3fn).view(np.uint8)
    else:
        c = by_word.astype(ml_dtypes.float4_e2m1fn).view(np.uint8) & 0xF
        words = (c[..., 0::2] | (c[..., 1::2] << 4)).reshape(k // 512, 128, 2 * n)
    return np.ascontiguousarray(words), np.ascontiguousarray(byte.astype(np.uint8).reshape(k // 512, 16, n))


def unpack_weight(words, scales, fmt):
    g, _, n = scales.shape
    words = np.ascontiguousarray(words).reshape(g, 128, n, -1)
    if fmt == "e4m3":
        vals = words.view(ml_dtypes.float8_e4m3fn).astype(np.float64)
    else:
        nib = np.empty((g, 128, n, 4), np.uint8)
        nib[..., 0::2] = words & 0xF
        nib[..., 1::2] = words >> 4
        vals = E2M1[nib]
    vals = vals * np.repeat(np.exp2(scales.astype(np.float64) - 127.0), 8, axis=1)[..., None]
    return vals.transpose(0, 1, 3, 2).reshape(g * 512, n)


K, T, E, C, N = 1024, 512, 8, 128, 256


def by_expert(wq, xq):
    return np.concatenate([wq[e].T @ xq[:, e * C:(e + 1) * C] for e in range(E)], axis=1)


def setup_inputs():
    n = np.random.standard_normal
    s = mx_kscale(K)[:, None]
    first = np.random.permutation(np.repeat(np.arange(E), T // E))
    second = (first + 1 + np.random.permutation(np.repeat(np.arange(E - 1), -(-T // (E - 1)))[:T])) % E
    while np.bincount(second, minlength=E).max() != T // E:
        load = np.bincount(second, minlength=E); hi, lo = int(load.argmax()), int(load.argmin())
        t = np.flatnonzero((second == hi) & (first != lo))[0]; second[t] = lo
    slot_token = np.empty(E * C, np.int64); pos = np.empty((2, T), np.int64); fill = np.zeros(E, np.int64)
    place = np.stack([np.random.permutation(C) for _ in range(E)])
    for r, deal in enumerate((first, second)):
        for t in np.random.permutation(T):
            e = deal[t]; j = e * C + place[e, fill[e]]; fill[e] += 1; slot_token[j] = t; pos[r, t] = j
    g = np.random.uniform(0.2, 0.8, T)
    w = [pack_weight(m, "e2m1") for m in n((E, K, N)) / np.sqrt(K) / s[None]]
    return {
        "xT": (n((K, T)) * s).astype(np.float32),
        "w_words": np.stack([m[0] for m in w]),
        "w_scales": np.stack([m[1] for m in w]),
        "gate": np.stack([np.tile(g, (N, 1)), np.tile(1.0 - g, (N, 1))]).astype(np.float32),
        "offs": striped(slot_token),
        "pos1": striped(pos[0]),
        "pos2": striped(pos[1]),
    }


def reference(xT, w_words, w_scales, gate, offs, pos1, pos2):
    idx = unstriped(offs)
    w = np.stack([unpack_weight(w_words[e], w_scales[e], "e2m1") for e in range(E)])
    xq = mxq(f64(xT)[:, idx], 0, "e4m3")
    y = by_expert(w, xq)
    return f64(gate[0]) * y[:, unstriped(pos1)] + f64(gate[1]) * y[:, unstriped(pos2)]

from contextlib import ExitStack

import concourse.mybir as mybir

F32 = mybir.dt.float32
BF16 = mybir.dt.bfloat16
I32 = mybir.dt.int32
U32 = mybir.dt.uint32
U16 = mybir.dt.uint16
U8 = mybir.dt.uint8
FP8X4 = mybir.dt.float8_e4m3fn_x4
FP4X4 = mybir.dt.float4_e2m1fn_x4
COPY = mybir.ActivationFunctionType.Copy
ADD = mybir.AluOpType.add
MULT = mybir.AluOpType.mult

P = 128
K, T, E, C, N = 1024, 512, 8, 128, 256
S = E * C
A = K // 512
H = N // P
FLOPS = 2 * K * N * S

TC = 256
W_WIDE = 1376
W_CUT = 1024
VEC_SHARE = (160, 160)
CUTS = (512, 256, 128, 128)


def tile_moe_pln_lin_none_kernel(tc, xT, w_words, w_scales, gate, offs, pos1, pos2, out):
    nc = tc.nc
    with ExitStack() as ctx:
        keep = ctx.enter_context(tc.tile_pool(name="keep", bufs=1))
        psum = ctx.enter_context(tc.psum_pool(name="psum", bufs=8))

        offs_sb = keep.tile([P, S // 16], U16, name="offs_sb")
        pos_sb = [keep.tile([P, T // 16], U16, name=f"pos{r}_sb") for r in range(2)]
        raw = [[keep.tile([P, 4, TC], F32, name=f"raw{a}_{c}") for c in range(T // TC)] for a in range(A)]
        xb = [[keep.tile([P, TC, 4], BF16, name=f"xb{a}_{c}", align_bytes=64) for c in range(T // TC)] for a in range(A)]
        words_w = (W_WIDE, W_CUT)
        xw = [keep.tile([P, words_w[a]], U32, name=f"xw{a}", align_bytes=64) for a in range(A)]
        xs = [keep.tile([P, W_WIDE], U8, name=f"xs{a}", align_bytes=64) for a in range(A)]
        gw = [keep.tile([P, S], U32, name=f"gw{a}", align_bytes=64) for a in range(A)]
        gs = [keep.tile([P, S], U8, name=f"gs{a}", align_bytes=64) for a in range(A)]
        wc = keep.tile([P, E * A, 2 * N], U8, name="wc", align_bytes=64)
        ws = keep.tile([P, E * A, N], U8, name="ws", align_bytes=64)
        gates = keep.tile([P, 2 * H, T], F32, name="gates")
        y = [keep.tile([P, S], F32, name=f"y{h}") for h in range(H)]
        prod = [[keep.tile([P, T], F32, name=f"prod{h}_{r}") for r in range(2)] for h in range(H)]
        res = [keep.tile([P, T], F32, name=f"res{h}") for h in range(H)]

        for a in range(A):
            rows = xT[512 * a : 512 * (a + 1), :].rearrange("(p j) t -> p j t", j=4)
            for c in range(T // TC):
                nc.sync.dma_start(raw[a][c][:], rows[:, :, TC * c : TC * (c + 1)])
            if a == 0:
                nc.sync.dma_start(offs_sb[:], offs)
        w_src = w_words.bitcast(I32).rearrange("e a p w -> p (e a) w")
        w_dst = wc[:].bitcast(I32)
        for half in range(2):
            sl = slice(E * half, E * (half + 1))
            nc.sync.dma_start(w_dst[:, sl, :], w_src[:, sl, :])

        nc.vector.memset(xw[0][:, T:].bitcast(I32), 0)
        for a in range(A):
            nc.vector.memset(xs[a][:].bitcast(I32), 0)
        nc.gpsimd.memset(ws[:].rearrange("p g n -> p (g n)").bitcast(I32), 0)
        nc.vector.memset(xw[1][:, T:].bitcast(I32), 0)

        s_src = w_scales.bitcast(I32).rearrange("e a (q r) n -> r q (e a) n", r=4)
        s_dst = ws[:].bitcast(I32)
        for r in range(4):
            nc.sync.dma_start(s_dst[r : P : 32, :, :], s_src[r])
        nc.sync.dma_start(pos_sb[0][:], pos1)
        nc.sync.dma_start(pos_sb[1][:], pos2)
        nc.sync.dma_start(gates[:], gate.rearrange("g (h p) t -> p (g h) t", p=P))

        def cast_and_quantise(a, c):
            v = VEC_SHARE[c] if a == 0 else 0
            src = raw[a][c][:].rearrange("p j t -> p t j")
            if v < TC:
                nc.scalar.activation(xb[a][c][:, v:, :], src[:, v:, :], COPY)
            if v > 0:
                nc.vector.tensor_copy(xb[a][c][:, :v, :], src[:, :v, :])
            cols = slice(TC * c, TC * (c + 1))
            nc.vector.quantize_mx(
                out=xw[a][:, cols].bitcast(FP8X4),
                scales=xs[a][:, cols],
                in_=xb[a][c][:].rearrange("p t j -> p (t j)"),
            )

        def product(bank, cols, e, h, a):
            g = A * e + a
            slots = slice(C * e, C * (e + 1))
            nc.tensor.matmul_mx(
                out=bank[:, cols],
                lhsT=wc[:, g, 2 * P * h : 2 * P * (h + 1)].bitcast(FP4X4),
                lhsT_scale=ws[:, g, P * h : P * (h + 1)],
                rhs=gw[a][:, slots].bitcast(FP8X4),
                rhs_scale=gs[a][:, slots],
                start=(a == 0),
                stop=(a == A - 1),
            )

        for c in range(T // TC):
            cast_and_quantise(0, c)
        nc.vector.tensor_copy(gw[0][:], xw[0][:].indirect(offs_sb[:]))
        nc.vector.tensor_copy(gs[0][:], xs[0][:].indirect(offs_sb[:]))
        banks = []
        for e in range(E):
            bank = psum.tile([P, C], F32, name="bank")
            banks.append(bank)
            product(bank, slice(0, C), e, 0, 0)

        for c in range(T // TC):
            cast_and_quantise(1, c)
        nc.vector.tensor_copy(gs[1][:], xs[1][:].indirect(offs_sb[:]))
        s0 = 0
        for width in CUTS:
            s1 = s0 + width
            nc.vector.tensor_copy(gw[1][:, s0:s1], xw[1][:].indirect(offs_sb[:, s0 // 16 : s1 // 16]))
            for e in range(s0 // C, s1 // C):
                product(banks[e], slice(0, C), e, 0, 1)
                nc.scalar.activation(y[0][:, C * e : C * (e + 1)], banks[e][:], COPY)
            s0 = s1
        for q in range(2):
            bank = psum.tile([P, 4 * C], F32, name="bank")
            for i in range(4):
                for a in range(A):
                    product(bank, slice(C * i, C * (i + 1)), 4 * q + i, 1, a)
            nc.scalar.activation(y[1][:, 4 * C * q : 4 * C * (q + 1)], bank[:], COPY)

        for h in range(H):
            for r in range(2):
                nc.vector.tensor_tensor(prod[h][r][:], y[h][:].indirect(pos_sb[r][:]), gates[:, H * r + h, :], MULT)
            nc.vector.tensor_tensor(res[h][:], prod[h][0][:], prod[h][1][:], ADD)
            nc.sync.dma_start(out[P * h : P * (h + 1), :], res[h][:])
